import numpy as np
import ml_dtypes


def mxq(x, axis, fmt="e4m3"):
    dtype, down = {"e4m3": (ml_dtypes.float8_e4m3fn, 7), "e5m2": (ml_dtypes.float8_e5m2, 14)}[fmt]
    v = np.moveaxis(np.asarray(x, np.float32).astype(ml_dtypes.bfloat16).astype(np.float64), axis, -1)
    blocks = v.reshape(v.shape[:-1] + (-1, 32))
    amax = np.abs(blocks).max(-1, keepdims=True)
    byte = np.maximum(np.where(amax > 0, np.frexp(amax)[1] - 1 + 127, 0) - down, 1)
    scale = np.exp2(byte - 127.0)
    codes = (blocks / scale).astype(np.float32).astype(dtype).astype(np.float64)
    return np.moveaxis((codes * scale).reshape(v.shape), -1, axis)


WIDE = False


def mx_kscale(k):
    if not WIDE:
        return np.ones(k)
    levels = np.array([30, -30])
    if k % 512:
        return np.exp2(np.random.permutation(np.resize(levels, k // 32))).repeat(32)
    a = np.empty((k // 512, 16))
    for p in range(k // 512):
        a[p, :8] = np.random.permutation(np.resize(levels, 8))
        for g in range(8):
            far = levels[np.abs(levels - a[p, g]) >= 10]
            a[p, g + 8] = far[np.random.randint(len(far))]
    return np.exp2(a.ravel()).repeat(32)


def f64(x):
    return np.asarray(x).astype(np.float64)


def striped(idx):
    return np.tile(np.asarray(idx).reshape(-1, 16).T, (8, 1)).astype(np.uint16)


def unstriped(offs):
    return offs[:16].T.reshape(-1).astype(np.int64)


E2M1 = np.array([0.0, 0.5, 1.0, 1.5, 2.0, 3.0, 4.0, 6.0, -0.0, -0.5, -1.0, -1.5, -2.0, -3.0, -4.0, -6.0])


def pack_weight(w, fmt):
    k, n = w.shape
    w = f64(np.asarray(w, np.float32).astype(ml_dtypes.bfloat16)).reshape(k // 32, 32, n)
    amax = np.abs(w).max(1)
    if fmt in ("e4m3", "e5m2"):
        byte = np.frexp(amax)[1] - 1 + 127 - (7 if fmt == "e4m3" else 14)
    else:
        mant, ex = np.frexp(amax / 6.0)
        byte = np.where(mant > 0.5, ex, ex - 1) + 127
    byte = np.clip(np.where(amax > 0, byte, 1), 1, 254)
    scaled = (w * np.exp2(127.0 - byte)[:, None, :]).reshape(k, n).astype(np.float32)
    by_word = np.ascontiguousarray(scaled.reshape(k // 512, 128, 4, n).transpose(0, 1, 3, 2))
    if fmt in ("e4m3", "e5m2"):
        words = by_word.astype(ml_dtypes.float8_e4m3fn if fmt == "e4m3" else ml_dtypes.float8_e5m2).view(np.uint8)
    else:
        c = by_word.astype(ml_dtypes.float4_e2m1fn).view(np.uint8) & 0xF
        words = (c[..., 0::2] | (c[..., 1::2] << 4)).reshape(k // 512, 128, 2 * n)
    return np.ascontiguousarray(words), np.ascontiguousarray(byte.astype(np.uint8).reshape(k // 512, 16, n))


def unpack_weight(words, scales, fmt):
    g, _, n = scales.shape
    words = np.ascontiguousarray(words).reshape(g, 128, n, -1)
    if fmt in ("e4m3", "e5m2"):
        vals = words.view(ml_dtypes.float8_e4m3fn if fmt == "e4m3" else ml_dtypes.float8_e5m2).astype(np.float64)
    else:
        nib = np.empty((g, 128, n, 4), np.uint8)
        nib[..., 0::2] = words & 0xF
        nib[..., 1::2] = words >> 4
        vals = E2M1[nib]
    vals = vals * np.repeat(np.exp2(scales.astype(np.float64) - 127.0), 8, axis=1)[..., None]
    return vals.transpose(0, 1, 3, 2).reshape(g * 512, n)


K, T, J, R, F, V, N = 512, 512, 256, 512, 512, 512, 256


def setup_inputs():
    n = np.random.standard_normal
    idx = np.random.permutation(T)[:J]
    idx2 = np.random.permutation(V)[:J]
    fk = mx_kscale(K)
    fr = mx_kscale(R)
    ff = mx_kscale(F)
    xtp = pack_weight(n((K, T)) / fk[:, None], "e4m3")
    wp = pack_weight(n((K, R)) * 1 / np.sqrt(K) * fk[:, None] * fr, "e5m2")
    sxp = pack_weight(n((F, J)) / ff[:, None], "e5m2")
    w2p = pack_weight(n((F, R)) * 1 / np.sqrt(F) * ff[:, None] * fr, "e4m3")
    wbp = pack_weight(n((R, N)) * 1 / np.sqrt(R) / fr[:, None], "e2m1")
    return {
        "xt_words": xtp[0],
        "xt_scales": xtp[1],
        "w_words": wp[0],
        "w_scales": wp[1],
        "sx_words": sxp[0],
        "sx_scales": sxp[1],
        "w2_words": w2p[0],
        "w2_scales": w2p[1],
        "tb": (n((R, V)) * 0.7 * fr[:, None]).astype(np.float32),
        "wb_words": wbp[0],
        "wb_scales": wbp[1],
        "bi": (np.random.uniform(-0.5, 0.5, (1, N))).astype(np.float32),
        "offs": striped(idx),
        "offs2": striped(idx2),
    }


def reference(xt_words, xt_scales, w_words, w_scales, sx_words, sx_scales, w2_words, w2_scales, tb, wb_words, wb_scales, bi, offs, offs2):
    idx = unstriped(offs)
    idx2 = unstriped(offs2)
    xtu = unpack_weight(xt_words, xt_scales, "e4m3")
    wu = unpack_weight(w_words, w_scales, "e5m2")
    sxu = unpack_weight(sx_words, sx_scales, "e5m2")
    w2u = unpack_weight(w2_words, w2_scales, "e4m3")
    wbu = unpack_weight(wb_words, wb_scales, "e2m1")
    xtidxg = xtu[:, idx]
    a = wu.T @ xtidxg + w2u.T @ sxu
    hid = np.maximum(a, f64(tb)[:, idx2])
    hidq = mxq(hid, 0, "e5m2")
    p = hidq.T @ wbu
    ea = np.exp(0.7 * p + f64(bi))
    y = 256.0 * ea / np.sum(ea, axis=1, keepdims=True)
    return y

@@ -1,0 +1,166 @@
+from contextlib import ExitStack
+
+import concourse.mybir as mybir
+from concourse.masks import make_identity
+
+K, T, J, R, F, V, N = 512, 512, 256, 512, 512, 512, 256
+FLOPS = 2 * K * R * J + 2 * F * R * J + 2 * R * J * N
+
+F32 = mybir.dt.float32
+BF16 = mybir.dt.bfloat16
+I32 = mybir.dt.int32
+U32 = mybir.dt.uint32
+U16 = mybir.dt.uint16
+U8 = mybir.dt.uint8
+E4M3 = mybir.dt.float8_e4m3fn_x4
+E5M2 = mybir.dt.float8_e5m2_x4
+E2M1 = mybir.dt.float4_e2m1fn_x4
+ALU = mybir.AluOpType
+ACT = mybir.ActivationFunctionType
+AX = mybir.AxisListType
+
+P = 128
+PACK = 4
+HALVES = J // P
+ROWS = 16
+
+
+def tile_list_sum_picked_own_abovetable_rowshares_kernel(
+    tc, xt_words, xt_scales, w_words, w_scales, sx_words, sx_scales, w2_words, w2_scales,
+    tb, wb_words, wb_scales, bi, offs, offs2, out,
+):
+    nc = tc.nc
+
+    def words(ap):
+        return ap[0].rearrange("p n t -> p (n t)").bitcast(I32)
+
+    with ExitStack() as ctx:
+        sb = ctx.enter_context(tc.tile_pool(name="sb", bufs=1))
+        ps = ctx.enter_context(tc.psum_pool(name="ps", bufs=1))
+
+        x_list = sb.tile([P, J // 16], U16, name="x_list")
+        tb_list = sb.tile([P, J // 16], U16, name="tb_list")
+        x_words = sb.tile([P, T], I32, name="x_words", align_bytes=64)
+        x_bytes = sb.tile([P, T], U8, name="x_bytes", align_bytes=64)
+        w_bytes = sb.tile([P, 2, R], U8, name="w_bytes", align_bytes=64)
+        plane = sb.tile([P, 2 * R + 2 * J + N], U8, name="plane", align_bytes=64)
+        wb_plane = plane[:, 2 * R + 2 * J :]
+        w_plane = [plane[:, 0:R], plane[:, R : 2 * R]]
+        x_plane = plane[:, 2 * R : 2 * R + J]
+        sx_plane = plane[:, 2 * R + J : 2 * R + 2 * J]
+
+        nc.vector.memset(w_bytes[:].rearrange("p s c -> p (s c)").bitcast(I32), 0)
+        nc.vector.memset(x_bytes[:].bitcast(I32), 0)
+        nc.gpsimd.memset(plane[:, 2 * R + J :].bitcast(I32), 0)
+
+        nc.sync.dma_start(x_list[:], offs)
+        nc.sync.dma_start(x_words[:], words(xt_words))
+        nc.scalar.dma_start(w_bytes[0:ROWS, 0, :].bitcast(I32), w_scales[0].bitcast(I32))
+        nc.scalar.dma_start(w_bytes[0:ROWS, 1, :].bitcast(I32), w2_scales[0].bitcast(I32))
+        nc.scalar.dma_start(x_bytes[0:ROWS, :].bitcast(I32), xt_scales[0].bitcast(I32))
+        nc.scalar.dma_start(plane[0:ROWS, 2 * R + J : 2 * R + 2 * J].bitcast(I32), sx_scales[0].bitcast(I32))
+        nc.sync.dma_start(tb_list[:], offs2)
+        tb_rows = tb.rearrange("(p t) v -> p t v", t=PACK)
+        tb_tiles = [sb.tile([P, 2, V], F32, name=f"tb_tile{u}") for u in range(2)]
+        for u in range(2):
+            nc.sync.dma_start(tb_tiles[u][:], tb_rows[:, 2 * u : 2 * u + 2, :])
+        w_raw = [sb.tile([P, R], I32, name=f"w_raw{s}") for s in range(2)]
+        nc.sync.dma_start(w_raw[0][:], words(w_words))
+        nc.sync.dma_start(w_raw[1][:], words(w2_words))
+        s_words = sb.tile([P, J], I32, name="s_words", align_bytes=64)
+        nc.sync.dma_start(s_words[:], words(sx_words))
+        wb_codes = sb.tile([P, 2 * N], U8, name="wb_codes", align_bytes=64)
+        nc.sync.dma_start(wb_codes[:].bitcast(I32), wb_words[0].bitcast(I32))
+
+        bias_col = sb.tile([P, 2], F32, name="bias_col")
+        nc.gpsimd.dma_start(plane[0:ROWS, 2 * R + 2 * J :].bitcast(I32), wb_scales[0].bitcast(I32))
+        nc.gpsimd.dma_start(bias_col[:], bi[0].rearrange("(p c) -> p c", c=2))
+        ident = sb.tile([P, P], F32, name="ident")
+        make_identity(nc, ident[:])
+
+        nc.vector.tensor_copy(
+            plane[:, 0 : 2 * R].rearrange("p (s t m) -> p s t m", s=2, t=PACK),
+            w_bytes[:].rearrange("p s (m t) -> p s t m", t=PACK),
+        )
+        xg_bytes = sb.tile([P, J], U8, name="xg_bytes", align_bytes=64)
+        nc.vector.tensor_copy(xg_bytes[:], x_bytes[:].indirect(x_list[:]))
+        nc.vector.tensor_copy(x_plane.bitcast(I32), xg_bytes[:].bitcast(I32))
+        for q in range(1, 4):
+            nc.scalar.dma_start(plane[32 * q : 32 * q + 4, :].bitcast(I32), plane[4 * q : 4 * q + 4, :].bitcast(I32))
+
+        xg_words = sb.tile([P, J], U32, name="xg_words", align_bytes=64)
+        nc.vector.tensor_copy(xg_words[:], x_words[:].bitcast(U32).indirect(x_list[:]))
+        w_dealt = [sb.tile([P, PACK, P], I32, name=f"w_dealt{s}", align_bytes=64) for s in range(2)]
+        for s in range(2):
+            nc.vector.tensor_copy(
+                w_dealt[s][:].rearrange("p t (c i) -> p c t i", i=4),
+                w_raw[s][:].rearrange("p (c i t) -> p c t i", i=4, t=PACK),
+            )
+
+        picked = sb.tile([P, PACK, J], F32, name="picked")
+        for t in range(PACK):
+            nc.scalar.activation(picked[:, t, :], tb_tiles[t // 2][:, t % 2, :].indirect(tb_list[:]), ACT.Copy)
+
+        bias_ps = ps.tile([P, 2, P], F32, name="bias_ps")
+        for c in range(2):
+            nc.tensor.transpose(bias_ps[:, c, :], bias_col[:, c : c + 1].to_broadcast([P, P]), ident[:])
+        bias = sb.tile([P, N], F32, name="bias")
+        nc.scalar.copy(bias[:].rearrange("p (n c) -> p n c", c=2), bias_ps[:].rearrange("p c n -> p n c"))
+
+        acc = [ps.tile([P, PACK, P], F32, name=f"acc{h}") for h in range(HALVES)]
+        moving = [(xg_words, x_plane, E4M3, E5M2), (s_words, sx_plane, E5M2, E4M3)]
+        for s in range(2):
+            codes, scales, moving_dt, weight_dt = moving[s]
+            for h in range(HALVES):
+                cols = slice(h * P, (h + 1) * P)
+                for t in range(PACK):
+                    nc.tensor.matmul_mx(
+                        out=acc[h][:, t, :],
+                        lhsT=w_dealt[s][:, t, :].bitcast(weight_dt),
+                        lhsT_scale=w_plane[s][:, t * P : (t + 1) * P],
+                        rhs=codes[:, cols].bitcast(moving_dt),
+                        rhs_scale=scales[:, cols],
+                        start=(s == 0 and t == 0),
+                        stop=(s == 1 and t == PACK - 1),
+                    )
+
+        logits = []
+        for h in range(HALVES):
+            cols = slice(h * P, (h + 1) * P)
+            hid = sb.tile([P, P, PACK], BF16, name=f"hid{h}", align_bytes=64)
+            nc.vector.tensor_tensor(
+                hid[:].rearrange("p (c i) t -> p c t i", i=2),
+                acc[h][:].rearrange("p t (c i) -> p c t i", i=2),
+                picked[:, :, cols].rearrange("p t (c i) -> p c t i", i=2),
+                ALU.max,
+            )
+            hid_codes = sb.tile([P, P], U32, name=f"hid_codes{h}", align_bytes=64)
+            hid_plane = sb.tile([P, P], U8, name=f"hid_plane{h}", align_bytes=64)
+            nc.vector.quantize_mx(
+                out=hid_codes[:].bitcast(E5M2), scales=hid_plane[:], in_=hid[:].rearrange("p j t -> p (j t)")
+            )
+            prod = ps.tile([P, N], F32, name=f"prod{h}")
+            nc.tensor.matmul_mx(
+                out=prod[:],
+                lhsT=hid_codes[:].bitcast(E5M2),
+                lhsT_scale=hid_plane[:],
+                rhs=wb_codes[:].bitcast(E2M1),
+                rhs_scale=wb_plane,
+                start=True,
+                stop=True,
+            )
+            logits.append(prod)
+
+        for h in range(HALVES):
+            neg = sb.tile([P, N], F32, name=f"neg{h}")
+            nc.vector.scalar_tensor_tensor(neg[:], logits[h][:], -0.7, bias[:], ALU.mult, ALU.subtract)
+            low = sb.tile([P, 1], F32, name=f"low{h}")
+            nc.vector.tensor_reduce(low[:], neg[:], AX.X, ALU.min)
+            ea = sb.tile([P, N], F32, name=f"ea{h}")
+            total = sb.tile([P, 1], F32, name=f"total{h}")
+            nc.scalar.activation(ea[:], neg[:], ACT.Exp, bias=low[:], scale=-1.0, accum_out=total[:])
+            inv = sb.tile([P, 1], F32, name=f"inv{h}")
+            nc.vector.reciprocal(inv[:], total[:])
+            res = sb.tile([P, N], F32, name=f"res{h}")
+            nc.vector.tensor_scalar(res[:], ea[:], inv[:], 256.0, ALU.mult, ALU.mult)
+            nc.sync.dma_start(out[h * P : (h + 1) * P, :], res[:])

@@ -42,51 +42,53 @@ def tile_list_sum_picked_own_abovetable_rowshares_kernel(
         tb_list = sb.tile([P, J // 16], U16, name="tb_list")
         x_words = sb.tile([P, T], I32, name="x_words", align_bytes=64)
         x_bytes = sb.tile([P, T], U8, name="x_bytes", align_bytes=64)
-        w_bytes = sb.tile([P, 2, R], U8, name="w_bytes", align_bytes=64)
-        plane = sb.tile([P, 2 * R + 2 * J + N], U8, name="plane", align_bytes=64)
-        wb_plane = plane[:, 2 * R + 2 * J :]
-        w_plane = [plane[:, 0:R], plane[:, R : 2 * R]]
-        x_plane = plane[:, 2 * R : 2 * R + J]
-        sx_plane = plane[:, 2 * R + J : 2 * R + 2 * J]
+        w_bytes = sb.tile([P, R], U8, name="w_bytes", align_bytes=64)
+        staged = sb.tile([P, R + 2 * J], U8, name="staged", align_bytes=64)
+        plane = sb.tile([P, 2, R + 2 * J], U8, name="plane", align_bytes=64)
+        w_plane = [plane[:, 0, 0:R], plane[:, 1, 0:R]]
+        sx_plane = plane[:, 0, R : R + J]
+        wb_plane = plane[:, 1, R : R + J]
+        x_plane = plane[:, 0, R + J :]
 
-        nc.vector.memset(w_bytes[:].rearrange("p s c -> p (s c)").bitcast(I32), 0)
         nc.vector.memset(x_bytes[:].bitcast(I32), 0)
-        nc.gpsimd.memset(plane[:, 2 * R + J :].bitcast(I32), 0)
+        nc.vector.memset(w_bytes[32:64, :].bitcast(I32), 0)
+        nc.vector.memset(w_bytes[64:128, :].bitcast(I32), 0)
 
-        nc.sync.dma_start(x_list[:], offs)
-        nc.sync.dma_start(x_words[:], words(xt_words))
-        nc.scalar.dma_start(w_bytes[0:ROWS, 0, :].bitcast(I32), w_scales[0].bitcast(I32))
-        nc.scalar.dma_start(w_bytes[0:ROWS, 1, :].bitcast(I32), w2_scales[0].bitcast(I32))
-        nc.scalar.dma_start(x_bytes[0:ROWS, :].bitcast(I32), xt_scales[0].bitcast(I32))
-        nc.scalar.dma_start(plane[0:ROWS, 2 * R + J : 2 * R + 2 * J].bitcast(I32), sx_scales[0].bitcast(I32))
-        nc.sync.dma_start(tb_list[:], offs2)
-        tb_rows = tb.rearrange("(p t) v -> p t v", t=PACK)
-        tb_tiles = [sb.tile([P, 2, V], F32, name=f"tb_tile{u}") for u in range(2)]
-        for u in range(2):
-            nc.sync.dma_start(tb_tiles[u][:], tb_rows[:, 2 * u : 2 * u + 2, :])
+        table = sb.tile([P, PACK, V], F32, name="table")
         w_raw = [sb.tile([P, R], I32, name=f"w_raw{s}") for s in range(2)]
-        nc.sync.dma_start(w_raw[0][:], words(w_words))
-        nc.sync.dma_start(w_raw[1][:], words(w2_words))
         s_words = sb.tile([P, J], I32, name="s_words", align_bytes=64)
-        nc.sync.dma_start(s_words[:], words(sx_words))
         wb_codes = sb.tile([P, 2 * N], U8, name="wb_codes", align_bytes=64)
-        nc.sync.dma_start(wb_codes[:].bitcast(I32), wb_words[0].bitcast(I32))
-
         bias_col = sb.tile([P, 2], F32, name="bias_col")
-        nc.gpsimd.dma_start(plane[0:ROWS, 2 * R + 2 * J :].bitcast(I32), wb_scales[0].bitcast(I32))
-        nc.gpsimd.dma_start(bias_col[:], bi[0].rearrange("(p c) -> p c", c=2))
         ident = sb.tile([P, P], F32, name="ident")
         make_identity(nc, ident[:])
+        nc.vector.memset(plane[:].rearrange("p s c -> p (s c)").bitcast(I32), 0)
+        even, odd = slice(0, 2 * ROWS, 2), slice(1, 2 * ROWS, 2)
+        nc.sync.dma_start(x_list[:], offs)
+        nc.scalar.dma_start(x_bytes[even, :].bitcast(I32), xt_scales[0].bitcast(I32))
+        nc.sync.dma_start(w_bytes[even, :].bitcast(I32), w_scales[0].bitcast(I32))
+        nc.sync.dma_start(w_bytes[odd, :].bitcast(I32), w2_scales[0].bitcast(I32))
+        nc.sync.dma_start(x_words[:], words(xt_words))
+        nc.sync.dma_start(staged[even, R : R + J].bitcast(I32), sx_scales[0].bitcast(I32))
+        nc.sync.dma_start(staged[odd, R : R + J].bitcast(I32), wb_scales[0].bitcast(I32))
+        nc.sync.dma_start(table[:], tb.rearrange("(p t) v -> p t v", t=PACK))
+        nc.sync.dma_start(tb_list[:], offs2)
+        nc.sync.dma_start(w_raw[0][:], words(w_words))
+        nc.sync.dma_start(w_raw[1][:], words(w2_words))
+        nc.gpsimd.dma_start(bias_col[:], bi[0].rearrange("(p c) -> p c", c=2))
+        nc.gpsimd.dma_start(wb_codes[:].bitcast(I32), wb_words[0].bitcast(I32))
+        nc.gpsimd.dma_start(s_words[:], words(sx_words))
 
-        nc.vector.tensor_copy(
-            plane[:, 0 : 2 * R].rearrange("p (s t m) -> p s t m", s=2, t=PACK),
-            w_bytes[:].rearrange("p s (m t) -> p s t m", t=PACK),
-        )
         xg_bytes = sb.tile([P, J], U8, name="xg_bytes", align_bytes=64)
         nc.vector.tensor_copy(xg_bytes[:], x_bytes[:].indirect(x_list[:]))
-        nc.vector.tensor_copy(x_plane.bitcast(I32), xg_bytes[:].bitcast(I32))
-        for q in range(1, 4):
-            nc.scalar.dma_start(plane[32 * q : 32 * q + 4, :].bitcast(I32), plane[4 * q : 4 * q + 4, :].bitcast(I32))
+        nc.vector.tensor_copy(
+            staged[:, 0:R].rearrange("p (t m) -> p t m", t=PACK),
+            w_bytes[:].rearrange("p (m t) -> p t m", t=PACK),
+        )
+        nc.vector.tensor_copy(staged[:, R + J :].bitcast(I32), xg_bytes[:].bitcast(I32))
+        for q in range(4):
+            (nc.scalar if q % 2 else nc.sync).dma_start(
+                plane[32 * q : 32 * q + 4, :, :].bitcast(I32), staged[8 * q : 8 * q + 8, :].bitcast(I32)
+            )
 
         xg_words = sb.tile([P, J], U32, name="xg_words", align_bytes=64)
         nc.vector.tensor_copy(xg_words[:], x_words[:].bitcast(U32).indirect(x_list[:]))
@@ -97,9 +99,11 @@ def tile_list_sum_picked_own_abovetable_rowshares_kernel(
                 w_raw[s][:].rearrange("p (c i t) -> p c t i", i=4, t=PACK),
             )
 
-        picked = sb.tile([P, PACK, J], F32, name="picked")
-        for t in range(PACK):
-            nc.scalar.activation(picked[:, t, :], tb_tiles[t // 2][:, t % 2, :].indirect(tb_list[:]), ACT.Copy)
+        picked = [sb.tile([P, PACK, P], F32, name=f"picked{h}") for h in range(HALVES)]
+        for h in range(HALVES):
+            entries = tb_list[:, h * (P // 16) : (h + 1) * (P // 16)]
+            for t in range(PACK):
+                nc.scalar.activation(picked[h][:, t, :], table[:, t, :].indirect(entries), ACT.Copy)
 
         bias_ps = ps.tile([P, 2, P], F32, name="bias_ps")
         for c in range(2):
@@ -109,10 +113,10 @@ def tile_list_sum_picked_own_abovetable_rowshares_kernel(
 
         acc = [ps.tile([P, PACK, P], F32, name=f"acc{h}") for h in range(HALVES)]
         moving = [(xg_words, x_plane, E4M3, E5M2), (s_words, sx_plane, E5M2, E4M3)]
-        for s in range(2):
-            codes, scales, moving_dt, weight_dt = moving[s]
-            for h in range(HALVES):
-                cols = slice(h * P, (h + 1) * P)
+        for h in range(HALVES):
+            cols = slice(h * P, (h + 1) * P)
+            for s in range(2):
+                codes, scales, moving_dt, weight_dt = moving[s]
                 for t in range(PACK):
                     nc.tensor.matmul_mx(
                         out=acc[h][:, t, :],
@@ -126,12 +130,11 @@ def tile_list_sum_picked_own_abovetable_rowshares_kernel(
 
         logits = []
         for h in range(HALVES):
-            cols = slice(h * P, (h + 1) * P)
             hid = sb.tile([P, P, PACK], BF16, name=f"hid{h}", align_bytes=64)
             nc.vector.tensor_tensor(
                 hid[:].rearrange("p (c i) t -> p c t i", i=2),
                 acc[h][:].rearrange("p t (c i) -> p c t i", i=2),
-                picked[:, :, cols].rearrange("p t (c i) -> p c t i", i=2),
+                picked[h][:].rearrange("p t (c i) -> p c t i", i=2),
                 ALU.max,
             )
             hid_codes = sb.tile([P, P], U32, name=f"hid_codes{h}", align_bytes=64)

@@ -54,7 +54,7 @@ def tile_list_sum_picked_own_abovetable_rowshares_kernel(
         nc.vector.memset(w_bytes[32:64, :].bitcast(I32), 0)
         nc.vector.memset(w_bytes[64:128, :].bitcast(I32), 0)
 
-        table = sb.tile([P, PACK, V], F32, name="table")
+        table = [sb.tile([P, 2, V], F32, name="table0")]
         w_raw = [sb.tile([P, R], I32, name=f"w_raw{s}") for s in range(2)]
         s_words = sb.tile([P, J], I32, name="s_words", align_bytes=64)
         wb_codes = sb.tile([P, 2 * N], U8, name="wb_codes", align_bytes=64)
@@ -63,22 +63,23 @@ def tile_list_sum_picked_own_abovetable_rowshares_kernel(
         make_identity(nc, ident[:])
         nc.vector.memset(plane[:].rearrange("p s c -> p (s c)").bitcast(I32), 0)
         even, odd = slice(0, 2 * ROWS, 2), slice(1, 2 * ROWS, 2)
+        tb_rows = tb.rearrange("(p t) v -> p t v", t=PACK)
         nc.sync.dma_start(x_list[:], offs)
-        nc.scalar.dma_start(x_bytes[even, :].bitcast(I32), xt_scales[0].bitcast(I32))
-        nc.sync.dma_start(w_bytes[even, :].bitcast(I32), w_scales[0].bitcast(I32))
+        nc.scalar.dma_start(w_bytes[even, :].bitcast(I32), w_scales[0].bitcast(I32))
         nc.sync.dma_start(w_bytes[odd, :].bitcast(I32), w2_scales[0].bitcast(I32))
-        nc.sync.dma_start(x_words[:], words(xt_words))
-        nc.sync.dma_start(staged[even, R : R + J].bitcast(I32), sx_scales[0].bitcast(I32))
+        nc.scalar.dma_start(staged[even, R : R + J].bitcast(I32), sx_scales[0].bitcast(I32))
         nc.sync.dma_start(staged[odd, R : R + J].bitcast(I32), wb_scales[0].bitcast(I32))
-        nc.sync.dma_start(table[:], tb.rearrange("(p t) v -> p t v", t=PACK))
+        nc.scalar.dma_start(x_bytes[even, :].bitcast(I32), xt_scales[0].bitcast(I32))
+        nc.sync.dma_start(x_words[:], words(xt_words))
+        nc.sync.dma_start(table[0][:], tb_rows[:, 0:2, :])
         nc.sync.dma_start(tb_list[:], offs2)
         nc.sync.dma_start(w_raw[0][:], words(w_words))
         nc.sync.dma_start(w_raw[1][:], words(w2_words))
+        nc.sync.dma_start(s_words[:], words(sx_words))
         nc.gpsimd.dma_start(bias_col[:], bi[0].rearrange("(p c) -> p c", c=2))
         nc.gpsimd.dma_start(wb_codes[:].bitcast(I32), wb_words[0].bitcast(I32))
-        nc.gpsimd.dma_start(s_words[:], words(sx_words))
 
-        xg_bytes = sb.tile([P, J], U8, name="xg_bytes", align_bytes=64)
+        xg_bytes = sb.tile([P, J], U8, name="xg_bytes", tag="second", align_bytes=64)
         nc.vector.tensor_copy(xg_bytes[:], x_bytes[:].indirect(x_list[:]))
         nc.vector.tensor_copy(
             staged[:, 0:R].rearrange("p (t m) -> p t m", t=PACK),
@@ -89,6 +90,8 @@ def tile_list_sum_picked_own_abovetable_rowshares_kernel(
             (nc.scalar if q % 2 else nc.sync).dma_start(
                 plane[32 * q : 32 * q + 4, :, :].bitcast(I32), staged[8 * q : 8 * q + 8, :].bitcast(I32)
             )
+        table.append(sb.tile([P, 2, V], F32, name="table1", tag="second", align_bytes=64))
+        nc.sync.dma_start(table[1][:], tb_rows[:, 2:4, :])
 
         xg_words = sb.tile([P, J], U32, name="xg_words", align_bytes=64)
         nc.vector.tensor_copy(xg_words[:], x_words[:].bitcast(U32).indirect(x_list[:]))
@@ -103,7 +106,11 @@ def tile_list_sum_picked_own_abovetable_rowshares_kernel(
         for h in range(HALVES):
             entries = tb_list[:, h * (P // 16) : (h + 1) * (P // 16)]
             for t in range(PACK):
-                nc.scalar.activation(picked[h][:, t, :], table[:, t, :].indirect(entries), ACT.Copy)
+                window = table[t // 2][:, t % 2, :].indirect(entries)
+                if t < 2 or (h, t) == (0, 2):
+                    nc.vector.tensor_copy(picked[h][:, t, :], window)
+                else:
+                    nc.scalar.activation(picked[h][:, t, :], window, ACT.Copy)
 
         bias_ps = ps.tile([P, 2, P], F32, name="bias_ps")
         for c in range(2):

@@ -55,9 +55,8 @@ def tile_list_sum_picked_own_abovetable_rowshares_kernel(
         nc.vector.memset(w_bytes[64:128, :].bitcast(I32), 0)
 
         table = [sb.tile([P, 2, V], F32, name="table0")]
-        w_raw = [sb.tile([P, R], I32, name=f"w_raw{s}") for s in range(2)]
+        w_raw = [sb.tile([P, R], I32, name=f"w_raw{s}", tag=f"w_raw{s}", align_bytes=64) for s in range(2)]
         s_words = sb.tile([P, J], I32, name="s_words", align_bytes=64)
-        wb_codes = sb.tile([P, 2 * N], U8, name="wb_codes", align_bytes=64)
         bias_col = sb.tile([P, 2], F32, name="bias_col")
         ident = sb.tile([P, P], F32, name="ident")
         make_identity(nc, ident[:])
@@ -77,7 +76,6 @@ def tile_list_sum_picked_own_abovetable_rowshares_kernel(
         nc.sync.dma_start(w_raw[1][:], words(w2_words))
         nc.sync.dma_start(s_words[:], words(sx_words))
         nc.gpsimd.dma_start(bias_col[:], bi[0].rearrange("(p c) -> p c", c=2))
-        nc.gpsimd.dma_start(wb_codes[:].bitcast(I32), wb_words[0].bitcast(I32))
 
         xg_bytes = sb.tile([P, J], U8, name="xg_bytes", tag="second", align_bytes=64)
         nc.vector.tensor_copy(xg_bytes[:], x_bytes[:].indirect(x_list[:]))
@@ -101,6 +99,8 @@ def tile_list_sum_picked_own_abovetable_rowshares_kernel(
                 w_dealt[s][:].rearrange("p t (c i) -> p c t i", i=4),
                 w_raw[s][:].rearrange("p (c i t) -> p c t i", i=4, t=PACK),
             )
+        wb_codes = sb.tile([P, 2 * N], U8, name="wb_codes", tag="w_raw0", align_bytes=64)
+        nc.sync.dma_start(wb_codes[:].bitcast(I32), wb_words[0].bitcast(I32))
 
         picked = [sb.tile([P, PACK, P], F32, name=f"picked{h}") for h in range(HALVES)]
         for h in range(HALVES):

from contextlib import ExitStack

import concourse.mybir as mybir
from concourse.masks import make_identity

K, T, J, R, F, V, N = 512, 512, 256, 512, 512, 512, 256
FLOPS = 2 * K * R * J + 2 * F * R * J + 2 * R * J * N

F32 = mybir.dt.float32
BF16 = mybir.dt.bfloat16
I32 = mybir.dt.int32
U32 = mybir.dt.uint32
U16 = mybir.dt.uint16
U8 = mybir.dt.uint8
E4M3 = mybir.dt.float8_e4m3fn_x4
E5M2 = mybir.dt.float8_e5m2_x4
E2M1 = mybir.dt.float4_e2m1fn_x4
ALU = mybir.AluOpType
ACT = mybir.ActivationFunctionType
AX = mybir.AxisListType

P = 128
PACK = 4
HALVES = J // P
ROWS = 16


def tile_list_sum_picked_own_abovetable_rowshares_kernel(
    tc, xt_words, xt_scales, w_words, w_scales, sx_words, sx_scales, w2_words, w2_scales,
    tb, wb_words, wb_scales, bi, offs, offs2, out,
):
    nc = tc.nc

    def words(ap):
        return ap[0].rearrange("p n t -> p (n t)").bitcast(I32)

    with ExitStack() as ctx:
        sb = ctx.enter_context(tc.tile_pool(name="sb", bufs=1))
        ps = ctx.enter_context(tc.psum_pool(name="ps", bufs=1))

        x_list = sb.tile([P, J // 16], U16, name="x_list")
        tb_list = sb.tile([P, J // 16], U16, name="tb_list")
        x_words = sb.tile([P, T], I32, name="x_words", align_bytes=64)
        x_bytes = sb.tile([P, T], U8, name="x_bytes", align_bytes=64)
        w_bytes = sb.tile([P, R], U8, name="w_bytes", align_bytes=64)
        staged = sb.tile([P, R + 2 * J], U8, name="staged", align_bytes=64)
        plane = sb.tile([P, 2, R + 2 * J], U8, name="plane", align_bytes=64)
        w_plane = [plane[:, 0, 0:R], plane[:, 1, 0:R]]
        sx_plane = plane[:, 0, R : R + J]
        wb_plane = plane[:, 1, R : R + J]
        x_plane = plane[:, 0, R + J :]

        nc.vector.memset(x_bytes[:].bitcast(I32), 0)
        nc.vector.memset(w_bytes[32:64, :].bitcast(I32), 0)
        nc.vector.memset(w_bytes[64:128, :].bitcast(I32), 0)

        table = [sb.tile([P, 2, V], F32, name="table0")]
        w_raw = [sb.tile([P, R], I32, name=f"w_raw{s}", tag=f"w_raw{s}", align_bytes=64) for s in range(2)]
        s_words = sb.tile([P, J], I32, name="s_words", align_bytes=64)
        bias_col = sb.tile([P, 2], F32, name="bias_col")
        ident = sb.tile([P, P], F32, name="ident")
        make_identity(nc, ident[:])
        nc.vector.memset(plane[:].rearrange("p s c -> p (s c)").bitcast(I32), 0)
        even, odd = slice(0, 2 * ROWS, 2), slice(1, 2 * ROWS, 2)
        tb_rows = tb.rearrange("(p t) v -> p t v", t=PACK)
        nc.sync.dma_start(x_list[:], offs)
        nc.scalar.dma_start(w_bytes[even, :].bitcast(I32), w_scales[0].bitcast(I32))
        nc.sync.dma_start(w_bytes[odd, :].bitcast(I32), w2_scales[0].bitcast(I32))
        nc.scalar.dma_start(staged[even, R : R + J].bitcast(I32), sx_scales[0].bitcast(I32))
        nc.sync.dma_start(staged[odd, R : R + J].bitcast(I32), wb_scales[0].bitcast(I32))
        nc.scalar.dma_start(x_bytes[even, :].bitcast(I32), xt_scales[0].bitcast(I32))
        nc.sync.dma_start(x_words[:], words(xt_words))
        nc.sync.dma_start(table[0][:], tb_rows[:, 0:2, :])
        nc.sync.dma_start(tb_list[:], offs2)
        nc.sync.dma_start(w_raw[0][:], words(w_words))
        nc.sync.dma_start(w_raw[1][:], words(w2_words))
        nc.sync.dma_start(s_words[:], words(sx_words))
        nc.gpsimd.dma_start(bias_col[:], bi[0].rearrange("(p c) -> p c", c=2))

        xg_bytes = sb.tile([P, J], U8, name="xg_bytes", tag="second", align_bytes=64)
        nc.vector.tensor_copy(xg_bytes[:], x_bytes[:].indirect(x_list[:]))
        nc.vector.tensor_copy(
            staged[:, 0:R].rearrange("p (t m) -> p t m", t=PACK),
            w_bytes[:].rearrange("p (m t) -> p t m", t=PACK),
        )
        nc.vector.tensor_copy(staged[:, R + J :].bitcast(I32), xg_bytes[:].bitcast(I32))
        for q in range(4):
            (nc.scalar if q % 2 else nc.sync).dma_start(
                plane[32 * q : 32 * q + 4, :, :].bitcast(I32), staged[8 * q : 8 * q + 8, :].bitcast(I32)
            )
        table.append(sb.tile([P, 2, V], F32, name="table1", tag="second", align_bytes=64))
        nc.sync.dma_start(table[1][:], tb_rows[:, 2:4, :])

        xg_words = sb.tile([P, J], U32, name="xg_words", align_bytes=64)
        nc.vector.tensor_copy(xg_words[:], x_words[:].bitcast(U32).indirect(x_list[:]))
        w_dealt = [sb.tile([P, PACK, P], I32, name=f"w_dealt{s}", align_bytes=64) for s in range(2)]
        for s in range(2):
            nc.vector.tensor_copy(
                w_dealt[s][:].rearrange("p t (c i) -> p c t i", i=4),
                w_raw[s][:].rearrange("p (c i t) -> p c t i", i=4, t=PACK),
            )
        wb_codes = sb.tile([P, 2 * N], U8, name="wb_codes", tag="w_raw0", align_bytes=64)
        nc.sync.dma_start(wb_codes[:].bitcast(I32), wb_words[0].bitcast(I32))

        picked = [sb.tile([P, PACK, P], F32, name=f"picked{h}") for h in range(HALVES)]
        for h in range(HALVES):
            entries = tb_list[:, h * (P // 16) : (h + 1) * (P // 16)]
            for t in range(PACK):
                window = table[t // 2][:, t % 2, :].indirect(entries)
                if t < 2 or (h, t) == (0, 2):
                    nc.vector.tensor_copy(picked[h][:, t, :], window)
                else:
                    nc.scalar.activation(picked[h][:, t, :], window, ACT.Copy)

        bias_ps = ps.tile([P, 2, P], F32, name="bias_ps")
        for c in range(2):
            nc.tensor.transpose(bias_ps[:, c, :], bias_col[:, c : c + 1].to_broadcast([P, P]), ident[:])
        bias = sb.tile([P, N], F32, name="bias")
        nc.scalar.copy(bias[:].rearrange("p (n c) -> p n c", c=2), bias_ps[:].rearrange("p c n -> p n c"))

        acc = [ps.tile([P, PACK, P], F32, name=f"acc{h}") for h in range(HALVES)]
        moving = [(xg_words, x_plane, E4M3, E5M2), (s_words, sx_plane, E5M2, E4M3)]
        for h in range(HALVES):
            cols = slice(h * P, (h + 1) * P)
            for s in range(2):
                codes, scales, moving_dt, weight_dt = moving[s]
                for t in range(PACK):
                    nc.tensor.matmul_mx(
                        out=acc[h][:, t, :],
                        lhsT=w_dealt[s][:, t, :].bitcast(weight_dt),
                        lhsT_scale=w_plane[s][:, t * P : (t + 1) * P],
                        rhs=codes[:, cols].bitcast(moving_dt),
                        rhs_scale=scales[:, cols],
                        start=(s == 0 and t == 0),
                        stop=(s == 1 and t == PACK - 1),
                    )

        logits = []
        for h in range(HALVES):
            hid = sb.tile([P, P, PACK], BF16, name=f"hid{h}", align_bytes=64)
            nc.vector.tensor_tensor(
                hid[:].rearrange("p (c i) t -> p c t i", i=2),
                acc[h][:].rearrange("p t (c i) -> p c t i", i=2),
                picked[h][:].rearrange("p t (c i) -> p c t i", i=2),
                ALU.max,
            )
            hid_codes = sb.tile([P, P], U32, name=f"hid_codes{h}", align_bytes=64)
            hid_plane = sb.tile([P, P], U8, name=f"hid_plane{h}", align_bytes=64)
            nc.vector.quantize_mx(
                out=hid_codes[:].bitcast(E5M2), scales=hid_plane[:], in_=hid[:].rearrange("p j t -> p (j t)")
            )
            prod = ps.tile([P, N], F32, name=f"prod{h}")
            nc.tensor.matmul_mx(
                out=prod[:],
                lhsT=hid_codes[:].bitcast(E5M2),
                lhsT_scale=hid_plane[:],
                rhs=wb_codes[:].bitcast(E2M1),
                rhs_scale=wb_plane,
                start=True,
                stop=True,
            )
            logits.append(prod)

        for h in range(HALVES):
            neg = sb.tile([P, N], F32, name=f"neg{h}")
            nc.vector.scalar_tensor_tensor(neg[:], logits[h][:], -0.7, bias[:], ALU.mult, ALU.subtract)
            low = sb.tile([P, 1], F32, name=f"low{h}")
            nc.vector.tensor_reduce(low[:], neg[:], AX.X, ALU.min)
            ea = sb.tile([P, N], F32, name=f"ea{h}")
            total = sb.tile([P, 1], F32, name=f"total{h}")
            nc.scalar.activation(ea[:], neg[:], ACT.Exp, bias=low[:], scale=-1.0, accum_out=total[:])
            inv = sb.tile([P, 1], F32, name=f"inv{h}")
            nc.vector.reciprocal(inv[:], total[:])
            res = sb.tile([P, N], F32, name=f"res{h}")
            nc.vector.tensor_scalar(res[:], ea[:], inv[:], 256.0, ALU.mult, ALU.mult)
            nc.sync.dma_start(out[h * P : (h + 1) * P, :], res[:])
